import numpy as np, ml_dtypes
CORES = [24,25,26,27,28,29,30,31]
N = 8
import mx_ref
BF = ml_dtypes.bfloat16
def gcols(t, e):
    v = np.concatenate([t.reshape(8, 16, -1, 4), np.zeros((8, 16, 1, 4), BF)], axis=2)
    return np.ascontiguousarray(np.stack([v[g][:, e[g]] for g in range(8)])).reshape(128, -1)
def tile(rs):
    return np.stack(rs, axis=2).reshape(128, -1).astype(BF)
def pick(q, e):
    c = np.concatenate([q[0].reshape(128, -1, 4), np.zeros((128, 1, 4), np.uint8)], axis=1); s = np.concatenate([q[1], np.ones((16, 1), np.uint8)], axis=1)
    return (np.ascontiguousarray(c[:, e].reshape(128, -1)), np.ascontiguousarray(s[:, e]))
def join(*qs):
    return (np.concatenate([q[0] for q in qs], axis=1), np.concatenate([q[1] for q in qs], axis=1))
def put(q, e, v):
    c, s = q[0].reshape(128, -1, 4).copy(), q[1].copy(); c[:, e] = v[0].reshape(128, -1, 4); s[:, e] = v[1]
    return (c.reshape(128, -1), s)
def pk(c, s):
    return (np.ascontiguousarray(c), mx_ref.live(s))
def emit(q):
    return q[0], q[1]
def packed(v, rng):
    q = [mx_ref.quantize(np.ascontiguousarray(v[r])) for r in range(N)]
    return np.stack([a for a, b in q]), np.stack([mx_ref.plane(b, rng) for a, b in q])
def f(rng, *shape):
    return mx_ref.flush((rng.standard_normal(shape, dtype=np.float32) * np.exp2(rng.integers(-2, 3, shape[:-1] + (1,)))).astype(BF))
def wide(rng, *shape, cols=0):
    v = rng.standard_normal(shape, dtype=np.float32) * np.exp2(rng.integers(-12, 13, shape)).astype(np.float32)
    if cols: v *= np.repeat(np.exp2(rng.integers(-cols, cols + 1, shape[:-2] + (1, shape[-1] // 4))) * (rng.random(shape[:-2] + (1, shape[-1] // 4)) > 0.0625), 4, axis=-1).astype(np.float32)
    return mx_ref.flush(v.astype(BF))
C, K, R = 256, 32, 2
STEP = [1, 6]
def runs(p):
    here, beside = [], []
    for g in range(8):
        a, s = p[16 * g] + np.float32(0.0), p[16 * g + 1] + np.float32(0.0)
        b = np.append(0, np.sort(1 + np.argsort(-s[1:], kind="stable")[:K - 1]))
        n = np.diff(np.append(b, C))
        e = []
        for i in range(K):
            k = b[i] + np.argsort(-a[b[i]:b[i] + n[i]], kind="stable")[:2]
            e += [(-a[k[0]], k[0], 0, i), (-a[k[-1]], k[-1], 1, i)]
        e = [(q[1], b[q[3]], n[q[3]]) for q in sorted(e)]
        h, m = [], []
        for (k, i, l), (k2, i2, l2) in zip(e, e[1:] + e[:1]):
            o = np.arange(l)
            h.append(i + (k - i + o) % l)
            m.append(i2 + (k2 - i2 + o) % l2)
        here.append(np.concatenate(h))
        beside.append(np.concatenate(m))
    return np.stack(here), np.stack(beside)
def big(v):
    v = v.astype(np.float32)
    v[np.abs(v) < np.float32(2.0 ** -16)] = 0
    return v.astype(BF)
def numbers_of(rng):
    return {"x": big(f(rng, N, 128, 4 * C)), "u": np.array(f(rng, N, 128, 512)), "v": np.array(f(rng, N, 128, 512))}
def weights(rng, still=[]):
    w = np.array(f(rng, N, 128, 2048)).reshape(N, 8, 16, 4, 8, 16, 4)
    for i in still:
        w[:, :, i] = 0
        w[:, :, :, :, :, i] = 0
    c, p = packed(w.reshape(N, 128, 2048), rng)
    return {"wc": c, "ws": p}
def signs(rng):
    return np.stack([rng.permutation(8) % 2 * 2.0 - 1.0 for r in range(N)])
def setup_inputs(rng):
    return {**numbers_of(rng), **weights(rng)}
def setup_inputs_ties(rng):
    d = numbers_of(rng)
    e = rng.permutation(N)
    x = d["x"].reshape(N, 8, 16, C, 4)
    for r in range(N):
        k = np.zeros(C, int) if r == e[0] else rng.permutation(C) % 3
        a = x[r][:, :8, :3].copy()
        a[:, :, 2] = 0
        x[r][:, :8] = a[:, :, k]
    x[e[1]] = 0
    u = d["u"].reshape(N, 8, 16, 8, 16, 4)
    k = u.copy()
    u[:, :, :, :, :2] = 0
    for g in range(8): u[:, g, :8, g, :2] = k[:, g, :8, g, :2]
    return {"x": x.reshape(N, 128, 4 * C), "u": u.reshape(N, 128, 512), "v": d["v"], **weights(rng, range(8))}
def setup_inputs_near(rng):
    d = numbers_of(rng)
    x = np.zeros((N, 8, 16, C, 4), np.float32)
    u = d["u"].reshape(N, 128, 128, 4)
    u[:, :, ::16] = 0
    u[:, :, 1::16] = 0
    kind, c = rng.permutation(N) % 4, [signs(rng), signs(rng)]
    j = np.arange(C)
    for r in range(N):
        size = 1.0 if kind[r] < 2 else 2.0 ** -4
        k = 1.0 if kind[r] == 0 else 2.0 ** -30
        l = C // 2 if kind[r] == 3 else C
        for row in range(2):
            if row == 0: i = (j + rng.integers(0, C, (8, 1))) % l
            else:
                i = (j + 8 * rng.integers(0, C // 8, (8, 1))) % l
                i = i % 8 * (l // 8) + i // 8
            s = i if kind[r] == 3 else (i + 1 - row) // 2
            z = ((s[:, :, None] >> np.arange(8)) & 1) * np.exp2(np.arange(8) - 23.0) * size
            if kind[r] < 2:
                x[r, :, row, :, 0] = c[row][r][:, None]
                for g in rng.permutation(8)[:4]: x[r, g, row, rng.integers(1, C), 0] *= np.float32(2.0 ** 30)
            if kind[r] == 3: x[r, :, row, :, 0] = (8 + j // (C // 2)) * 2.0 ** -30
            x[r, :, 8 + 2 * row] = z[:, :, :4]
            x[r, :, 9 + 2 * row] = z[:, :, 4:]
            for h in range(0, 128, 16):
                u[r, h + row, h + row, 0] = k
                u[r, h + 8 + 2 * row:h + 10 + 2 * row, h + row] = k
        x[r, :, 12:] = rng.integers(4, 8, (8, 4, C, 4)) * 2.0 ** -20 * size
    return {"x": x.reshape(N, 128, 4 * C).astype(BF), "u": u.reshape(N, 128, 512), "v": d["v"], **weights(rng, range(12))}
def setup_inputs_huge(rng):
    d = numbers_of(rng)
    c = np.stack([rng.permutation(C) % 2 * 2.0 - 1.0 for r in range(N)])
    c[rng.permutation(N) < N // 2] = -1
    x = 2.0 ** 30 * (0.6 + 0.2 * rng.random((N, 128, C, 4))) * c[:, None, :, None]
    u = d["u"].reshape(N, 128, 8, 16, 4)
    a = 2.0 ** 30 * (1 - 0.1 * rng.random((N, 128, 8, 2, 4))) * np.stack([signs(rng), signs(rng)], axis=2)[:, None, :, :, None]
    u[:, :, :, :2] = a.astype(np.float32).astype(BF)
    w = np.zeros((N, 128, 4, 128, 4), np.float32)
    i = np.arange(128)
    for b in range(4): w[:, i, b, i, b] = -1
    wc, ws = packed(w.reshape(N, 128, 2048).astype(BF), rng)
    return {"x": x.astype(np.float32).reshape(N, 128, 4 * C).astype(BF), "u": u.reshape(N, 128, 512), "v": d["v"], "wc": wc, "ws": ws}
def setup_inputs_cuts(rng):
    d = numbers_of(rng)
    x = d["x"].reshape(N, 8, 16, C, 4)
    u = d["u"].reshape(N, 128, 128, 4)
    x[:, :, 0] = 0
    u[:, :, 1::16] = 0
    u[:, ::16, ::16, 1] = 0
    for h in range(0, 128, 16):
        u[:, h, h + 1, 0] = 1
        u[:, h, h, 1] = 1024
    m = np.arange(1, K)
    end = [C - 1, C - K, C - K + K // 2 - 1]
    for r in range(N):
        way = [m, C - m, np.where(m < K // 2, m, C - K + m), 2 * m, 3 * m, C // K * m, 1 + rng.permutation(C - 1)[:K - 1], np.append([1, C - 1], 2 + rng.permutation(C - 3)[:K - 3])]
        top, last = rng.permutation(8) % 2, rng.permutation(3)
        for g, i in enumerate(rng.permutation(8)):
            s = -1.0 * rng.integers(0, 3, C)
            s[way[i]] = rng.integers(8, 16, K - 1) * 0.125
            s[0] = 4.0 if top[g] else -4.0
            x[r, g, 0, :, 0] = s.astype(np.float32).astype(BF)
            if i < 3 and last[i] < 2:
                x[r, g, 0, end[i], 1] = 64
                if last[i] == 1: x[r, g, 0, end[i] - 1 - int(rng.integers(C - K)), 1] = 128
    return {"x": x.reshape(N, 128, 4 * C), "u": u.reshape(N, 128, 512), "v": d["v"], **weights(rng, [0])}
def setup_inputs_spread(rng):
    d = setup_inputs(rng)
    d["x"] = big(wide(rng, N, 128, 4 * C, cols=6))
    return d
def check_inputs(d):
    b = []
    for k in ("x", "u", "v"):
        a = np.abs(d[k].astype(np.float32))
        if not (np.isfinite(a).all() and ((a == 0) | (a >= 2.0 ** -30) & (a <= 2.0 ** 30)).all()): b.append("a value of " + k)
    if ((d["wc"] & 0x7F) == 0x7F).any(): b.append("a code of wc that is no number")
    z = np.zeros((128, 4, 4), np.float32)
    z[:, 1] = 2.0 ** -30
    z[:, 2] = 2.0 ** 30
    c, s = emit(mx_ref.quantize(z.reshape(128, 16).astype(BF)))
    for r in range(N):
        p = mx_ref.live(d["ws"][r])
        if not ((p == s[0, 0]) | (p >= s[0, 1]) & (p <= s[0, 2])).all(): b.append("a scale of ws")
    return b
def reference(x, u, v, wc, ws):
    qu = [mx_ref.quantize(u[r]) for r in range(N)]
    lay = [pk(wc[r], ws[r]) for r in range(N)]
    now = [x[r] for r in range(N)]
    for t in range(R):
        at, made = [], []
        for r in range(N):
            e, h = runs(mx_ref.matmul(qu[r], mx_ref.quantize(now[r])))
            z = ((gcols(now[r], e).astype(np.float32) + gcols(now[r], h).astype(np.float32)) * np.float32(0.5)).astype(BF)
            at.append(e)
            made.append(mx_ref.quantize(z))
        for r in range(N):
            q = join(pick(made[r], np.arange(C)), pick(made[r ^ STEP[t]], np.arange(C, 2 * C)))
            h = tile([mx_ref.matmul(pick(lay[r], np.arange(128 * b, 128 * b + 128)), q) * np.float32(0.03125) for b in range(4)])
            back = np.argsort(at[r], axis=1, kind="stable")
            s = gcols(h, back[:, ::2]).astype(np.float32) + gcols(h, back[:, 1::2]).astype(np.float32)
            now[r] = (s * np.float32(0.5) + now[r].astype(np.float32)).astype(BF)
    y, ol = np.zeros((N, 128, C), np.float32), np.zeros((N, 8, 2 * C), np.float32)
    oc, osc = np.zeros((N, 128, 4 * C), np.uint8), np.zeros((N, 16, C), np.uint8)
    for r in range(N):
        q = mx_ref.quantize(now[r])
        y[r] = mx_ref.matmul(mx_ref.quantize(v[r]), q)
        ol[r] = at[r]
        oc[r], osc[r] = emit(q)
    return {"y": y, "ol": ol, "oc": oc, "osc": osc}

from concourse.mybir import dt, AluOpType as Op, ActivationFunctionType as Fn

C = 256
STEP = [1, 6]
BIG = 2.0 ** 96
EPS = 2.0 ** -120
U = 1.0 / 512
RW = 288
KO = 528
WO = 129
RN, RKB, RE, RK, RH, RL, RO, RV = 0, 1, 2, 3, 4, 8, 12, 15

X4, U8, BF, F32, I32, U16, F16 = "float8_e4m3fn_x4", "uint8", "bfloat16", "float32", "int32", "uint16", "float16"
SCRATCH = {"ps": ("psum", [128, 4096], F32)}
for _n, _w, _d in [
    ("X0", 1024, BF), ("X1", 1024, BF), ("X2", 1024, BF), ("ub", 512, BF), ("vb", 512, BF),
    ("qu", 128, X4), ("su", 128, U8), ("qp", 384, X4), ("sp", 384, U8), ("qv", 128, X4), ("sv", 128, U8),
    ("wq", 512, X4), ("wp", 512, U8),
    ("qx0", 256, X4), ("sx0", 256, U8), ("qx1", 256, X4), ("sx1", 256, U8), ("qx2", 256, X4), ("sx2", 256, U8),
    ("qs0", 256, X4), ("ss0", 256, U8), ("qs1", 256, X4), ("ss1", 256, U8),
    ("ql0", 256, X4), ("sl0", 256, U8), ("ql1", 256, X4), ("sl1", 256, U8),
    ("qo", 256, X4), ("so", 256, U8),
    ("Za", 1024, BF), ("Zb", 1024, BF), ("Xh", 1024, BF), ("Hh", 2048, BF), ("gz", 2048, BF), ("hq", 1024, BF), ("sf", 1024, F32),
    ("PI", 8, I32), ("PJ", 8, I32), ("CF", 32, F32), ("FI", 96, F32), ("OF", 96, U16), ("DO", 32, U16), ("LF", 32, U16), ("LG", 32, U16), ("LQ", 32, U16),
    ("one", 528, BF), ("MSK", RW, BF), ("io32", 256, BF), ("Lc", 256, BF), ("KK", 8, F32), ("io16", 64, F32), ("m16", 64, F32),
    ("sg16", 64, F32), ("sg32", 256, BF), ("sg64", 256, BF), ("ioC", 256, BF), ("LcC", 256, BF), ("io4", 4, F32), ("cb", 4, F32),
    ("io2", WO + 512, F32), ("u1", 256, BF), ("u2", 256, BF), ("e32", 32, BF),
    ("n32i", 32, F32), ("N32", 32, F32), ("SG", 32, F32), ("nm", 32, F32), ("n1", 32, F32), ("rhi", 32, BF), ("IN", 512, F32), ("RT", 512, F32),
    ("ST", 256, F32), ("CC", 8 * RW, BF), ("SO", 8 * RW + 8, BF), ("S3", 2048, BF), ("jk", 2048, BF), ("acc", 16, F32),
    ("DG", 256, BF), ("DS", 256, BF), ("th", 16, F32), ("BC", 256, BF), ("R", 256, BF), ("tid", 256, BF), ("ac2", 4, F32),
    ("EB", 256, F32), ("W1", WO + 512, F32), ("W2", WO + 512, F32), ("nr", 256, BF), ("h2", 256, BF), ("D1", 256, F32),
    ("Q", 4, F32), ("tE", 64, F32), ("base", 64, F32), ("n4", 256, BF), ("Vm", 64, F32), ("Vr", 64, F32), ("VS", 64, F32),
    ("dd", 256, BF), ("bt", 256, BF), ("bw", 256, BF), ("PS", 256, F16), ("td", 64, F32), ("AT", 128, F32),
    ("SC", 2 * KO, BF), ("FB", 1056, BF), ("TT", 2080, BF), ("s1", 96, F32), ("sa", 128, F32), ("a1", 96, F32),
    ("gt", 128, F32), ("qi", 32, I32), ("ft", 96, F32), ("OL", 512, F32), ("iol", 512, F32),
    ("IN2", 128, F32), ("T2", 128, F32), ("AT2", 64, F32), ("SC2", 512, BF), ("kp2", 512, BF), ("FB2", 544, BF), ("TT2", 1056, BF),
    ("g2", 64, F32), ("pt", 128, F32), ("yb", 256, F32),
]:
    SCRATCH[_n] = ("sbuf", [128, _w], _d)
NDMA = 14
SEMAPHORES = ["cv", "ca", "cp", "cg", "arr0", "arr1", "sent"] + ["d%d" % _i for _i in range(NDMA)]


def V(name, lo=0, hi=None, st=1, p=None, cast=None, ind=None):
    if hi is None: hi = SCRATCH[name][1][1]
    return ("view", name, lo, hi, st, p, cast, ind)


def col(name, c):
    return V(name, c, c + 1)


def is_view(a):
    return isinstance(a, tuple) and len(a) == 8 and a[0] == "view"


def make(T, v):
    if not is_view(v): return v
    _, name, lo, hi, st, p, cast, ind = v
    cs = slice(lo, hi) if st == 1 else slice(lo, hi, st)
    if p is None: ap = T[name][:, cs]
    elif p[2] == 1: ap = T[name][p[0]:p[1], cs]
    else: ap = T[name][p[0]:p[1]:p[2], cs]
    if cast is not None: ap = ap.bitcast(cast)
    if ind is not None: ap = ap.indirect(make(T, ind))
    return ap


def region(v):
    _, name, lo, hi, st, p, cast, ind = v
    m = 0
    if name == "ps":
        for b in range(lo // 512, (hi - 1) // 512 + 1): m |= 1 << b
        return (name, m)
    if st == 1: m = ((1 << (hi - lo)) - 1) << lo
    else:
        for c in range(lo, hi, st): m |= 1 << c
    return (name, m)


def rank_program(g, core, T, topo):
    rank = T.rank_of(core)
    if rank is None: return
    ops = []

    def add(q, fn, outs, ins, kind="c", waits=()):
        rd, wr = [], []
        for v in ins:
            if is_view(v):
                rd.append(region(v))
                if v[7] is not None: rd.append(region(v[7]))
        for v in outs:
            if is_view(v):
                wr.append(region(v))
                if v[7] is not None: rd.append(region(v[7]))
        ops.append((q, fn, rd, wr, kind, list(waits)))

    def m(v): return make(T, v)
    def ts(o, i, s1, o0, s2=None, o1=None):
        if o1 is None: add("v", lambda: g.vector.tensor_scalar(m(o), m(i), m(s1), None, o0), [o], [i, s1])
        else: add("v", lambda: g.vector.tensor_scalar(m(o), m(i), m(s1), m(s2), o0, o1), [o], [i, s1, s2])
    def tt(o, a, b, op): add("v", lambda: g.vector.tensor_tensor(m(o), m(a), m(b), op), [o], [a, b])
    def cp(o, i): add("v", lambda: g.vector.tensor_copy(m(o), m(i)), [o], [i])
    def ms(o, c): add("v", lambda: g.vector.memset(m(o), c), [o], [])
    def tr(o, i): add("v", lambda: g.vector.transpose(m(o), m(i)), [o], [i])
    def rc(o, i): add("v", lambda: g.vector.reciprocal(m(o), m(i)), [o], [i])
    def sc(o, d0, d1, ini, o0, o1): add("v", lambda: g.vector.tensor_tensor_scan(m(o), m(d0), m(d1), m(ini), o0, o1), [o], [d0, d1, ini])
    def qz(q, s, i): add("v", lambda: g.vector.quantize_mx(m(q), m(s), m(i)), [q, s], [i])
    def act(o, i, f=Fn.Identity, bias=None, scale=None, acc=None):
        def run():
            kw = {}
            if bias is not None: kw["bias"] = m(bias)
            if scale is not None: kw["scale"] = m(scale)
            if acc is not None: kw["accum_out"] = m(acc)
            return g.scalar.activation(m(o), m(i), f, **kw)
        add("a", run, [o, acc], [i, bias, scale])
    def fill(o, n, c): act(o, V("one", 0, n), scale=c)
    def mm(o, w, ws, x, xs, waits=()):
        add("p", lambda: g.tensor.matmul_mx(m(o), m(w), m(ws), m(x), m(xs), True, True), [o], [w, ws, x, xs], "c", waits)
    def io(o, pat, base=0, cm=0):
        if SCRATCH[o[1]][2] == I32: add("g", lambda: g.iota(m(o), pat, base, cm), [o], [])
        else: add("g", lambda: g.iota(m(o), pat, base, cm, allow_small_or_imprecise_dtypes=True), [o], [])
    def sel(o, i, pat, cmp, fil, base, cm): add("g", lambda: g.affine_select(m(o), m(i), pat, cmp, fil, base, cm), [o], [i])
    def dma(q, o, i):
        e = {"s": g.sync, "a": g.scalar}[q]
        add(q, lambda: e.dma_start(m(o), m(i)), [o], [i], "d")
    def bank(b, lo=0, hi=C): return V("ps", 512 * b + lo, 512 * b + hi)

    dma("a", V("ub"), T.u[:])
    dma("s", V("X0"), T.x[:])
    add("s", None, [], [V("X0"), V("ub")], "w")
    dma("s", V("wq", cast=dt.uint8), T.wc[:])
    dma("s", V("wp"), T.ws[:])
    dma("s", V("vb"), T.v[:])

    I16, H16, J32, PAR, HLF, CE = [col("CF", c) for c in range(6)]
    A16, NE, C1, G1, G2, AL, CNT, I2, Z0, NP = [col("CF", c) for c in range(8, 18)]
    L_PICK, L_BC, L_DG = V("OF", 0, 24), V("OF", 24, 40), V("OF", 40, 56)
    L_S1, L_SA, L_A1 = V("OF", 56, 62), V("OF", 62, 70), V("OF", 70, 76)
    L_G2, L_Y2, L_T2 = V("OF", 76, 80), V("OF", 80, 82), V("OF", 82, 86)

    def clear_places():
        fill(V("SC", 0, KO), KO, CNT)
        fill(V("SC", KO, 2 * KO), KO, 1.0)

    io(V("PI"), [[0, 8]], 0, 1)
    io(V("n32i"), [[0, 2], [32, 8], [0, 2]])
    io(V("FI", 0, 16), [[16, 2], [32, 4], [0, 2]], 1)
    io(V("FI", 16, 24), [[16, 8]])
    io(V("FI", 24, 40, 2), [[RW, 8]], RW - 1)
    io(V("FI", 25, 40, 2), [[1, 8]], 8 * RW)
    io(V("FI", 40, 56), [[RW, 8], [16, 2]])
    io(V("io32"), [[0, 8], [1, 32]])
    io(V("FI", 56, 60), [[0, 2], [256, 2]], RO)
    io(V("FI", 60, 64), [[RN - RL, 2], [256, 2]], 512 + RL)
    io(V("FI", 64, 68), [[RN - RE, 2], [256, 2]], RE)
    io(V("FI", 68, 70), [[256, 2]], RV)
    io(V("FI", 70, 74), [[RK - RKB, 2], [256, 2]], 512 + RKB)
    io(V("FI", 74, 76), [[256, 2]], 512 + RH)
    io(V("FI", 76, 80), [[RO - RN, 2], [256, 2]], RN)
    io(V("FI", 80, 82), [[256, 2]], RKB)
    io(V("FI", 82, 86), [[32, 4]])
    io(V("io16"), [[0, 4], [1, 16]])
    io(V("io4"), [[1, 2], [16, 2]])
    for s in range(2): io(V("ioC", 128 * s, 128 * s + 128), [[-32, 2], [1, 2], [2, 32]], -s)
    ms(V("one"), 1.0)
    ts(col("PJ", 0), col("PI", 0), 15, Op.bitwise_and)
    ts(col("PJ", 1), col("PI", 0), 16, Op.bitwise_and)
    ts(col("PJ", 2), col("PI", 0), 31, Op.bitwise_and)
    ts(col("PJ", 3), col("PI", 0), 1, Op.bitwise_and)
    ts(col("PJ", 4), col("PI", 0), 15, Op.bitwise_and, 1, Op.logical_shift_right)
    ts(col("PJ", 5), col("PI", 0), 1, Op.logical_shift_right, 1, Op.bitwise_and)
    fill(V("IN"), 512, 0.0)
    fill(V("MSK"), RW, 1.0)
    cp(V("CF", 0, 6), V("PJ", 0, 6))
    ms(V("SG", 0, 16), 1.0)
    ms(V("acc"), 0.0)
    ms(col("EB", 0), -BIG)
    ts(V("N32"), V("n32i"), J32, Op.add)
    ts(NE, PAR, 16.0, Op.mult, H16, Op.not_equal)
    ts(CNT, I16, 11.5, Op.is_gt)
    ts(V("nm"), V("N32"), 1.0, Op.max)
    ts(V("SG", 16, 32), V("N32", 16, 32), 1.0, Op.is_equal, -1.0, Op.add)
    cp(V("OF", 0, 40), V("FI", 0, 40))
    rc(V("IN", RH, 512, 16), V("nm"))
    act(A16, HLF, bias=H16, scale=32.0)
    act(C1, PAR, bias=1024.0, scale=32.0)
    act(Z0, J32, Fn.Relu, bias=1.0, scale=-1.0)
    act(V("n1"), V("N32"), bias=-1.0)
    act(G1, C1, bias=A16, scale=NE)
    act(V("IN", RN, 512, 16), V("N32"))
    fill(V("IN", RE, 512, 16), 32, -255.0)
    act(V("IN", RV, 512, 16), V("SG"), bias=-256.0)
    act(V("IN", RK, 512, 16), V("SG"))
    act(I2, I16, scale=2.0)
    act(G2, NE, bias=G1, scale=-512.0)
    act(AL, PAR, scale=-512.0)
    act(NP, PAR, scale=-1.0)
    clear_places()
    ts(V("OF", 40, 56), V("FI", 40, 56), I16, Op.add)
    cp(V("rhi"), V("IN", RH, 512, 16))
    tt(V("IN", RKB, 512, 16), V("n1"), V("SG"), Op.add)
    tt(V("IN", RL, 512, 16), V("IN", RH, 512, 16), V("rhi"), Op.subtract)
    ts(V("Lc"), V("io32"), J32, Op.is_lt)
    ts(V("MSK", 1, 33), V("io32", 0, 32), J32, Op.not_equal)
    ts(V("e32"), V("io32", 0, 32), J32, Op.is_equal)
    ms(col("Lc", 0), -2.0)
    tr(V("RT"), V("IN"))
    qz(V("qu"), V("su"), V("ub"))
    act(V("sp"), V("su", ind=L_PICK), Fn.Copy)
    cp(V("qp", cast=dt.uint32), V("qu", cast=dt.uint32, ind=L_PICK))
    io(V("KK", 1, 8), [[-32, 7]], 0)
    io(V("CC", 2 * RW - 1, 8 * RW, RW), [[0, 7]], -3920)
    sel(V("sg32"), V("one", 0, 256), [[0, 8], [1, 32]], Op.not_equal, 0.0, 0, 0)
    io(col("D1", 0), [[0, 1]])
    for w in ("io2", "W1", "W2"): io(V(w, 0, WO), [[0, WO]])
    io(V("io2", WO), [[0, 2], [1, 256]])
    io(V("iol"), [[0, 2], [1, 256]])
    sel(V("sg16"), V("one", 0, 64), [[0, 4], [1, 16]], Op.not_equal, 0.0, 0, 0)
    sel(V("sg64"), V("one", 0, 256), [[0, 4], [1, 64]], Op.not_equal, 0.0, 0, 0)
    io(V("AT", 64, 128), [[0, 64]])
    io(V("IN2"), [[0, 128]])
    for o in (V("FB", 0, 16), V("FB", 1040, 1056), V("FB2", 0, 16), V("FB2", 528, 544)): io(o, [[0, 16]])

    def halve(X, t): act(V("Xh", 256 * t, 256 * t + 256), V(X, t, 1024, 4), scale=0.5)
    HS = 0.03125 * 0.5

    for r in range(2):
        X, Xn = "X%d" % r, "X%d" % (r + 1)
        qx, sx = V("qx%d" % r), V("sx%d" % r)
        peer = T.cores[rank ^ STEP[r]]
        qz(qx, sx, V(X))
        mm(bank(0), V("qu"), V("su"), qx, sx)
        for k in (1, 0, 2): mm(bank(1 + k), V("qp", 128 * k, 128 * k + 128), V("sp", 128 * k, 128 * k + 128), qx, sx)
        if r == 0:
            ts(V("OF", 56, 76), V("FI", 56, 76), G1, Op.add)
            ts(V("OF", 76, 82), V("FI", 76, 82), G2, Op.add)
            ts(V("OF", 82, 86), V("FI", 82, 86), J32, Op.add)
            ts(V("m16"), V("io16"), I16, Op.is_equal)
            act(V("MSK", 255, 287), V("e32"), bias=1.0, scale=127.0)
            act(col("CC", RW - 1), Z0, bias=-3920.0, scale=-61616.0)
            act(col("KK", 0), Z0, bias=31.0, scale=969.0)
            for t in range(2): halve(X, t)
        tr(V("ST"), bank(0))
        for b in range(8): act(V("S3", 256 * b, 256 * b + 256), bank(2), Fn.Sign, bias=col("ST", 32 * b + 17), scale=-1.0)
        for b in range(8):
            s, o, n = col("ST", 32 * b + 1), RW * b, C - 32 * b
            ts(V("CC", o, o + n), bank(1, 32 * b, C), s, Op.is_gt)
            ts(V("CC", o + n, o + RW - 1), bank(1, 1, 32 * b + 32), s, Op.is_ge)
        for b in range(7): act(V("jk", 256 * b + 32 * b + 32, 256 * b + 256), V("S3", 256 * b + 32 * b + 32, 256 * b + 256), Fn.Relu, scale=-1.0, acc=col("acc", b))
        for b in range(1, 8): act(V("jk", 256 * b + 1, 256 * b + 32 * b), V("S3", 256 * b + 1, 256 * b + 32 * b), Fn.Relu, acc=col("acc", 8 + b))
        tt(V("DG"), V("S3", ind=L_DG), V("Lc"), Op.is_lt)
        for b in range(8):
            sc(V("SO", RW * b, RW * b + RW), V("MSK"), V("CC", RW * b, RW * b + RW), 0.0, Op.mult, Op.add)
            if b == 0: sc(V("DS"), V("sg32"), V("DG"), 0.0, Op.mult, Op.add)
            if b == 2: tt(V("th", 0, 8), V("DS", 31, 256, 32), V("KK"), Op.subtract)
            if b == 5: tt(V("th", 8, 16), V("th", 0, 8), V("acc", 0, 8), Op.add)
        if r == 0:
            ts(V("cb"), V("io4"), I16, Op.add, 0.5, Op.add)
            fill(V("u1"), 256, U)
        tt(V("SO", 8 * RW, 8 * RW + 8), V("th", 8, 16), V("acc", 8, 16), Op.subtract)
        if r == 0:
            ts(V("LcC"), V("ioC"), I2, Op.is_lt, EPS, Op.mult)
            fill(V("u2"), 256, 2 * U)
        ts(V("BC"), V("SO", ind=L_BC), 0.0, Op.is_lt, -BIG, Op.mult)
        tr(V("R"), V("BC"))
        A = bank(3)
        LV, LN, LP, LB = V("DO", 0, 4), V("DO", 4, 8), V("DO", 8, 16), V("DO", 16, 20)
        sc(V("tid"), V("R"), V("R"), 0.0, Op.add, Op.min)
        sc(V("EB", 1, C), bank(3, 0, C - 1), V("R", 1, C), -BIG, Op.max, Op.add)
        for k in range(4): act(V("jk", 256 * k, 256 * k + 256), V("tid"), Fn.Sign, bias=col("cb", k), scale=1.0 / BIG, acc=col("ac2", k))
        sc(V("W1", WO, WO + C), V("R"), A, -BIG, Op.add, Op.max)
        tt(V("nr"), A, V("EB"), Op.is_le)
        sc(V("W1", WO + C, WO + 2 * C), A, V("EB"), -BIG, Op.max, Op.min)
        sc(V("W2", WO, WO + C), V("nr"), V("u1"), 0.0, Op.mult, Op.add)
        tt(V("Q", 0, 2), V("ac2", 2, 4), V("ac2", 0, 2), Op.subtract)
        ts(V("DO", 0, 2), V("ac2", 2, 4), 0.5, Op.mult, 127.0 + WO, Op.add)
        ts(V("Q", 2, 4), V("Q", 0, 2), 4.0, Op.min, 128.0, Op.mult)
        ts(V("DO", 4, 6), V("Q", 0, 2), 0.5, Op.mult)
        for k in range(2): ts(col("DO", 2 + k), col("ac2", 2 + k), 0.5, Op.mult, col("Q", 2 + k), Op.add)
        ts(V("DO", 6, 8), V("Q", 0, 2), 0.5, Op.mult, 256.0, Op.add)
        for s in range(2): act(V("kp2", 256 * s, 256 * s + 256), V("R"), Fn.Relu, bias=1.0, scale=1.0 / BIG)
        tt(V("Vm"), V("W1", ind=LV), V("m16"), Op.mult)
        act(V("Vr"), V("W1", ind=LV))
        tt(V("h2", 1, C), bank(3, 1, C), V("W1", WO + C, WO + 2 * C - 1), Op.is_le)
        sc(V("VS"), V("sg16"), V("Vm"), 0.0, Op.mult, Op.add)
        act(V("tE"), V("io2", ind=LV), scale=CE)
        for k in range(4): act(V("dd", 64 * k, 64 * k + 64), V("Vr"), bias=col("VS", 16 * k + 15), scale=-1.0)
        for k in range(4): act(V("n4", 64 * k, 64 * k + 64), V("iol", ind=LN))
        tt(V("D1", 1, C), V("h2", 1, C), V("W2", WO, WO + C - 1), Op.add)
        tt(V("bt"), V("dd"), V("LcC"), Op.is_lt)
        sc(V("W2", WO + C, WO + 2 * C), V("u2"), V("D1"), 0.0, Op.add, Op.min)
        act(V("td"), V("W2", ind=LV), scale=AL)
        tt(V("bw"), V("bt"), V("n4"), Op.mult)
        tt(V("base"), V("RT", ind=LN), V("tE"), Op.add)
        sc(V("PS"), V("sg64"), V("bw"), 0.0, Op.mult, Op.add)
        tt(V("AT", 0, 64), V("td"), V("base"), Op.add)
        P = V("PS", 63, 256, 64)
        cp(V("DO", 8, 12), P)
        ts(V("DO", 12, 16), P, float(KO), Op.add)
        tt(V("AT", 32, 64), V("AT", 32, 64), V("td", 0, 32), Op.subtract)
        ts(V("DO", 16, 18), V("ac2", 0, 2), 0.5, Op.mult, 128.0, Op.add)
        for y in range(2): act(V("IN2", 16 * y + RO, 128, 32), P, bias=-256.0)
        fill(V("SC2"), 512, NP)
        if r == 0:
            for t in range(2, 4): halve(X, t)
        cp(V("SC", ind=LP), V("AT"))
        ts(V("DO", 18, 20), V("ac2", 0, 2), 0.5, Op.mult, 384.0, Op.add)
        sc(V("FB", 16, 528), V("SC", KO, KO + 512), V("SC", 0, 512), 0.0, Op.mult, Op.add)
        sc(V("FB", 1039, 527, -1), V("SC", KO + 512, KO, -1), V("SC", 512, 0, -1), col("SC", 0), Op.mult, Op.add)
        tr(V("TT", 0, 1024), V("FB", 16, 1040))
        tr(V("TT", 1024, 2080), V("FB"))
        cp(V("s1"), V("TT", ind=L_S1))
        act(V("sa"), V("TT", ind=L_SA))
        tt(V("a1"), V("TT", ind=L_A1), V("s1"), Op.add)
        tt(V("ft", 0, 32), V("sa", 96, 128), V("sa", 32, 64), Op.is_ge)
        tt(V("gt", 0, 32), V("a1", 0, 32), V("a1", 64, 96), Op.mult)
        tt(V("ft", 32, 64), V("ft", 0, 32), V("sa", 64, 96), Op.mult)
        ts(V("qi"), V("gt", 0, 32), -0.498, Op.add)
        tt(V("ft", 64, 96), V("sa", 96, 128), V("ft", 32, 64), Op.subtract)
        tt(V("gt", 32, 64), V("qi"), V("sa", 0, 32), Op.mult)
        ts(V("LF"), V("ft", 64, 96), 256.0, Op.add)
        tt(V("gt", 64, 96), V("a1", 32, 64), V("gt", 32, 64), Op.subtract)
        tr(V("T2"), V("IN2"))
        cp(V("LG"), V("gt", 64, 96))
        tt(V("AT2"), V("T2", ind=L_T2), V("AT", 0, 64), Op.add)
        qs, ss, ql, sl = V("qs%d" % r), V("ss%d" % r), V("ql%d" % r), V("sl%d" % r)
        for h, Z in ((1, "Za"), (0, "Zb")):
            for t in range(4):
                z = V("gz", 1024 * h + 256 * t, 1024 * h + 256 * t + 256)
                act(z, V("Xh", 256 * t, 256 * t + 256, ind=V("LF", 16 * h, 16 * h + 16)))
                tt(V(Z, t, 1024, 4), V("Xh", 256 * t, 256 * t + 256, ind=V("LG", 16 * h, 16 * h + 16)), z, Op.add)
                if h == 1 and t == 3: cp(V("SC2", ind=LB), V("AT2"))
                if h == 0 and t == 3: sc(V("FB2", 16, 528), V("kp2"), V("SC2"), 0.0, Op.mult, Op.add)
            if h == 1:
                ops.insert(len(ops), ops.pop())
                qz(qs, ss, V(Z))
                ops[-1], ops[-2] = ops[-2], ops[-1]
                rid, pid, _e = topo.addr(peer)
                eng = topo.engines(core, peer)
                mc, mp = sum(1 << e for e in eng[0::2]), sum(1 << e for e in eng[1::2])
                got = len(eng)
                arr = T.sem["arr%d" % r]
                add("g", lambda a=(ql, qs, arr, pid, rid, mc): g.remote_dma(m(a[0]).bitcast(dt.uint8), m(a[1]).bitcast(dt.uint8), a[2], T.sem.sent, a[3], a[4], a[5]), [], [qs], "r")
                add("g", lambda a=(sl, ss, arr, pid, rid, mp): g.remote_dma(m(a[0]), m(a[1]), a[2], T.sem.sent, a[3], a[4], a[5]), [], [ss], "r")
            else: qz(V("qo"), V("so"), V(Z))
        if r == 0: clear_places()
        else:
            act(V("OL"), V("iol", ind=V("LF")))
            dma("s", T.ol[:], V("OL", p=(0, 128, 16)))
        wb = [(V("wq", 128 * b, 128 * b + 128), V("wp", 128 * b, 128 * b + 128)) for b in range(4)]
        for b in range(4): mm(bank(4 + b), wb[b][0], wb[b][1], V("qo"), V("so"))
        for b in range(4): mm(bank(b), wb[b][0], wb[b][1], ql, sl, [(arr, got)] if b == 0 else [])
        def ev(b, h, q):
            o, i = V("Hh", 512 * b + 256 * h, 512 * b + 256 * h + 256), bank(b if h else 4 + b)
            if q == "a": act(o, i, scale=HS)
            else: ts(o, i, HS, Op.mult)
        for b in range(4): ev(b, 0, "a")
        ev(0, 1, "a")
        tr(V("TT2", 0, 512), V("FB2", 16, 528))
        tr(V("TT2", 512, 1056), V("FB2"))
        cp(V("g2"), V("TT2", ind=L_G2))
        ts(V("pt", 0, 32), V("TT2", ind=L_Y2), 0.0, Op.is_gt)
        tt(V("pt", 32, 64), V("TT2", ind=L_Y2), V("g2", 32, 64), Op.subtract)
        tt(V("pt", 64, 96), V("pt", 0, 32), V("g2", 0, 32), Op.mult)
        if r == 0: qz(V("qv"), V("sv"), V("vb"))
        tt(V("pt", 96, 128), V("pt", 64, 96), V("pt", 32, 64), Op.subtract)
        ts(V("LQ"), V("pt", 96, 128), 256.0, Op.add)
        ev(1, 1, "v")
        ev(2, 1, "v")
        for b in range(4):
            hw = lambda l: V("Hh", 512 * b, 512 * b + 512, ind=l)
            q, s = V("hq", 256 * b, 256 * b + 256), V("sf", 256 * b, 256 * b + 256)
            if b == 3: ev(b, 1, "a")
            act(q, hw(V("LQ", 16, 32)))
            tt(s, hw(V("LQ", 0, 16)), q, Op.add)
            if b > 0: tt(V(Xn, b - 1, 1024, 4), V("sf", 256 * b - 256, 256 * b), V(X, b - 1, 1024, 4), Op.add)
        tt(V(Xn, 3, 1024, 4), V("sf", 768, 1024), V(X, 3, 1024, 4), Op.add)
        if r == 0:
            for t in range(4): halve(Xn, t)

    qz(V("qx2"), V("sx2"), V("X2"))
    mm(bank(4), V("qv"), V("sv"), V("qx2"), V("sx2"))
    dma("a", T.oc[:], V("qx2", cast=dt.uint8))
    for k in range(4): dma("a" if k % 2 else "s", T.osc[4 * k:4 * k + 4, :], V("sx2", p=(32 * k, 32 * k + 4, 1)))
    cp(V("yb"), bank(4))
    dma("s", T.y[:], V("yb"))

    queue = {"v": g.vector, "a": g.scalar, "p": g.tensor, "g": g, "s": g.sync}
    csem = {"v": T.sem.cv, "a": T.sem.ca, "p": T.sem.cp, "g": T.sem.cg}
    count = {k: 0 for k in csem}
    known = {k: {} for k in queue}
    done = []
    seen = {}
    nd = [0]
    for i, (q, fn, rd, wr, kind, waits) in enumerate(ops):
        need = set()
        for regs, mine in ((rd, False), (wr, True)):
            for (name, cm) in regs:
                for (j, w2, cm2) in seen.get(name, []):
                    if cm & cm2 and (mine or w2 or (name == "ps" and ops[j][0] != q)) and done[j] is not None: need.add(j)
        for j in sorted(need, reverse=True):
            key, cnt, kn = done[j]
            if known[q].get(key, 0) >= cnt: continue
            queue[q].wait_ge(csem[key] if key in csem else T.sem[key], cnt)
            known[q][key] = cnt
            for k2 in kn:
                if known[q].get(k2, 0) < kn[k2]: known[q][k2] = kn[k2]
        for (s, n) in waits: queue[q].wait_ge(s, n)
        if kind == "w":
            done.append(None)
            continue
        ins = fn()
        if kind == "c":
            count[q] += 1
            ins.then_inc(csem[q], 1)
            done.append((q, count[q], dict(known[q])))
        elif kind == "d":
            key = "d%d" % nd[0]
            nd[0] += 1
            ins.then_inc(T.sem[key], 16)
            done.append((key, 16, dict(known[q])))
        else: done.append(None)
        for regs, w in ((rd, False), (wr, True)):
            for (name, cm) in regs: seen.setdefault(name, []).append((i, w, cm))
    g.wait_ge(T.sem.sent, 2 * got)
    for k in csem: g.sync.wait_ge(csem[k], count[k])
    for k in range(nd[0]): g.sync.wait_ge(T.sem["d%d" % k], 16)
